import numpy as np
import ml_dtypes


def mxq(x, axis, fmt="e4m3"):
    dtype, down = {"e4m3": (ml_dtypes.float8_e4m3fn, 7), "e5m2": (ml_dtypes.float8_e5m2, 14)}[fmt]
    v = np.moveaxis(np.asarray(x, np.float32).astype(ml_dtypes.bfloat16).astype(np.float64), axis, -1)
    blocks = v.reshape(v.shape[:-1] + (-1, 32))
    amax = np.abs(blocks).max(-1, keepdims=True)
    byte = np.maximum(np.where(amax > 0, np.frexp(amax)[1] - 1 + 127, 0) - down, 1)
    scale = np.exp2(byte - 127.0)
    codes = (blocks / scale).astype(np.float32).astype(dtype).astype(np.float64)
    return np.moveaxis((codes * scale).reshape(v.shape), -1, axis)


WIDE = False


def mx_kscale(k):
    if not WIDE:
        return np.ones(k)
    levels = np.array([10, -10, 5, -5, 0])
    if k % 512:
        return np.exp2(np.random.permutation(np.resize(levels, k // 32))).repeat(32)
    a = np.empty((k // 512, 16))
    for p in range(k // 512):
        a[p, :8] = np.random.permutation(np.resize(levels, 8))
        for g in range(8):
            far = levels[np.abs(levels - a[p, g]) >= 10]
            a[p, g + 8] = far[np.random.randint(len(far))]
    return np.exp2(a.ravel()).repeat(32)


def f64(x):
    return np.asarray(x).astype(np.float64)


def striped(idx):
    return np.tile(idx.reshape(-1, 16).T, (8, 1)).astype(np.uint16)


def unstriped(offs):
    return offs[:16].T.reshape(-1).astype(np.int64)


def pack_weight(w):
    k, n = w.shape
    w = f64(np.asarray(w, np.float32).astype(ml_dtypes.bfloat16)).reshape(k // 32, 32, n)
    amax = np.abs(w).max(1)
    byte = np.clip(np.where(amax > 0, np.frexp(amax)[1] - 1 + 127 - 7, 1), 1, 254)
    scaled = (w * np.exp2(127.0 - byte)[:, None, :]).reshape(k, n).astype(np.float32)
    words = np.ascontiguousarray(scaled.reshape(k // 512, 128, 4, n).transpose(0, 1, 3, 2)).astype(ml_dtypes.float8_e4m3fn).view(np.uint8)
    return words, np.ascontiguousarray(byte.astype(np.uint8).reshape(k // 512, 16, n))


def unpack_weight(words, scales):
    g, p, n, _ = words.shape
    vals = np.ascontiguousarray(words).view(ml_dtypes.float8_e4m3fn).astype(np.float64) * np.repeat(np.exp2(scales.astype(np.float64) - 127.0), 8, axis=1)[..., None]
    return vals.transpose(0, 1, 3, 2).reshape(g * 512, n)


E2M1 = np.array([0.0, 0.5, 1.0, 1.5, 2.0, 3.0, 4.0, 6.0, -0.0, -0.5, -1.0, -1.5, -2.0, -3.0, -4.0, -6.0])


def pack_fp4(w):
    k, n = w.shape
    w = f64(np.asarray(w, np.float32).astype(ml_dtypes.bfloat16)).reshape(k // 32, 32, n)
    amax = np.abs(w).max(1)
    mant, ex = np.frexp(amax / 6.0)
    byte = np.clip(np.where(amax > 0, np.where(mant > 0.5, ex, ex - 1) + 127, 1), 1, 254)
    scaled = (w * np.exp2(127.0 - byte)[:, None, :]).reshape(k, n).astype(np.float32)
    c = np.ascontiguousarray(scaled.reshape(k // 512, 128, 4, n).transpose(0, 1, 3, 2)).astype(ml_dtypes.float4_e2m1fn).view(np.uint8) & 0xF
    words = (c[..., 0::2] | (c[..., 1::2] << 4)).reshape(k // 512, 128, 2 * n)
    return np.ascontiguousarray(words), np.ascontiguousarray(byte.astype(np.uint8).reshape(k // 512, 16, n))


def unpack_fp4(words, scales):
    g, _, n = scales.shape
    words = np.ascontiguousarray(words).reshape(g, 128, n, 2)
    nib = np.empty((g, 128, n, 4), np.uint8)
    nib[..., 0::2] = words & 0xF
    nib[..., 1::2] = words >> 4
    vals = E2M1[nib] * np.repeat(np.exp2(scales.astype(np.float64) - 127.0), 8, axis=1)[..., None]
    return vals.transpose(0, 1, 3, 2).reshape(g * 512, n)


def planes(y):
    n, m = y.shape
    v = y.astype(np.float32).astype(ml_dtypes.bfloat16).astype(np.float64).reshape(n // 32, 32, m)
    top = np.abs(v).max(1)
    byte = np.clip(np.where(top > 0, np.frexp(top)[1] - 1 + 127 - 7, 1), 1, 254)
    codes = (v * np.exp2(127.0 - byte)[:, None, :]).reshape(n, m).astype(np.float32).astype(ml_dtypes.float8_e4m3fn).view(np.uint8)
    words = codes.reshape(n // 512, 128, 4, m).transpose(0, 1, 3, 2)
    return np.ascontiguousarray(words), np.ascontiguousarray(byte.astype(np.uint8).reshape(n // 512, 16, m))


K, T, S, N, H, J, C = 512, 2048, 512, 512, 512, 512, 512


def setup_inputs():
    n = np.random.standard_normal
    s = mx_kscale(K)[:, None]
    u = mx_kscale(S)
    packed_xT = pack_weight(n((K, T)) * s)
    packed_w1 = pack_fp4(n((K, H)) / np.sqrt(K) / s)
    packed_w2 = pack_fp4(n((H, N)) / np.sqrt(H) / u[:, None])
    return {
        "x_words": packed_xT[0],
        "x_scales": packed_xT[1],
        "w1_words": packed_w1[0],
        "w1_scales": packed_w1[1],
        "tab": n((H, J)).astype(np.float32),
        "gn": (np.random.uniform(0.5, 1.5, (H, 1)) * u[:, None]).astype(np.float32),
        "w2_words": packed_w2[0],
        "w2_scales": packed_w2[1],
        "gs": (np.random.uniform(0.5, 1.5, (K, 1)) / s).astype(np.float32),
        "offs": striped(np.random.permutation(T)[:S]),
        "n1": striped(np.random.randint(0, J, S)),
        "n2": striped(np.random.permutation(S)),
        "n3": striped(np.random.permutation(S)),
        "n4": striped(np.random.permutation(S)),
        "n5": striped(np.random.permutation(S)),
        "cand": striped(np.random.permutation(T)[:C]),
        "n6": striped(np.random.permutation(S)),
        "n7": striped(np.random.permutation(S)),
    }


def reference(x_words, x_scales, w1_words, w1_scales, tab, gn, w2_words, w2_scales, gs, offs, n1, n2, n3, n4, n5, cand, n6, n7):
    xq = unpack_weight(x_words, x_scales)[:, unstriped(offs)]
    y = unpack_fp4(w1_words, w1_scales).T @ xq
    z = f64(gn) * (np.abs(y - y[:, unstriped(n2)] - f64(tab)[:, unstriped(n1)]))
    a = unpack_fp4(w2_words, w2_scales).T @ mxq(z, 0, "e4m3")
    x_cand = unpack_weight(x_words, x_scales)[:, unstriped(cand)]
    z2 = f64(gs) * (0.75 * (y * y[:, unstriped(n3)] + y[:, unstriped(n4)] * y[:, unstriped(n5)]))
    b = 0.0625 * ((x_cand.T @ mxq(z2, 0, "e4m3")))
    out_0 = np.maximum(a, b[:, unstriped(n7)]) - (np.minimum(a[:, unstriped(n6)], b))
    return (out_0,) + planes(out_0)

@@ -1,0 +1,292 @@
+from contextlib import ExitStack
+
+import concourse.mybir as mybir
+
+K, T, S = 512, 2048, 512
+FLOPS = 3 * 2 * 512 * 512 * 512
+
+F32 = mybir.dt.float32
+BF16 = mybir.dt.bfloat16
+I32 = mybir.dt.int32
+U32 = mybir.dt.uint32
+U16 = mybir.dt.uint16
+U8 = mybir.dt.uint8
+FP8X4 = mybir.dt.float8_e4m3fn_x4
+FP4X4 = mybir.dt.float4_e2m1fn_x4
+ALU = mybir.AluOpType
+ACT = mybir.ActivationFunctionType
+
+P = 128
+PACK = 4
+HALF = S // 2
+HALVES = 2
+
+
+def tile_picked_fkcdmaxbkindddot_none_po_kernel(
+    tc, x_words, x_scales, w1_words, w1_scales, tab, gn, w2_words, w2_scales, gs,
+    offs, n1, n2, n3, n4, n5, cand, n6, n7, out_0, out_1, out_2,
+):
+    nc = tc.nc
+
+    with ExitStack() as ctx:
+        lists = ctx.enter_context(tc.tile_pool(name="lists", bufs=1))
+        keep = ctx.enter_context(tc.tile_pool(name="keep", bufs=1))
+        psum = ctx.enter_context(tc.psum_pool(name="psum", bufs=1))
+
+        def cols(h):
+            return slice(h * HALF, (h + 1) * HALF)
+
+        def load_list(src, name):
+            tile = lists.tile([P, S // 16], U16, name=name)
+            nc.sync.dma_start(tile[:], src)
+            return tile
+
+        def part(lst, h):
+            return lst[:, h * HALF // 16 : (h + 1) * HALF // 16]
+
+        def load_scale_rows(queue, tile, src):
+            for q in range(4):
+                queue.dma_start(tile[32 * q : 32 * q + 4, :].bitcast(I32), src[0, 4 * q : 4 * q + 4, :].bitcast(I32))
+
+        def sbuf(shape, dtype, name, tag=None):
+            return keep.tile(shape, dtype, name=name, tag=tag or name, align_bytes=64)
+
+        def planes(name, tag=None):
+            return sbuf([P, PACK, S], F32, name, tag)
+
+        def windows(name):
+            return [sbuf([P, S], F32, name + str(t)) for t in range(PACK)]
+
+        def by_pairs(ap):
+            return ap.rearrange("p t (c i) -> p c t i", i=2)
+
+        def woven_by_pairs(tile):
+            return tile[:].rearrange("p (c i t) -> p c t i", i=2, t=PACK)
+
+        x_sc = sbuf([P, T], U8, "x_sc")
+        w1_sc = sbuf([P, S], U8, "w1_sc")
+        w2_sc = sbuf([P, S], U8, "w2_sc")
+        nc.vector.memset(x_sc[:, : T // 2].bitcast(I32), 0)
+        nc.gpsimd.memset(x_sc[:, T // 2 :].bitcast(I32), 0)
+        nc.gpsimd.memset(w1_sc[:].bitcast(I32), 0)
+        nc.gpsimd.memset(w2_sc[:].bitcast(I32), 0)
+
+        l_offs = load_list(offs, "l_offs")
+        l_cand = load_list(cand, "l_cand")
+        load_scale_rows(nc.sync, x_sc, x_scales)
+        x_w = sbuf([P, T], I32, "x_w")
+        nc.sync.dma_start(x_w[:], x_words[0].rearrange("p n r -> p (n r)").bitcast(I32))
+        w1_w = sbuf([P, 2 * S], U8, "w1_w")
+        nc.sync.dma_start(w1_w[:].bitcast(I32), w1_words[0].bitcast(I32))
+        load_scale_rows(nc.sync, w1_sc, w1_scales)
+        gs_sb = sbuf([P, PACK], F32, "gs_sb")
+        nc.sync.dma_start(gs_sb[:], gs.rearrange("(p t) o -> p (t o)", t=PACK))
+        l_n3 = load_list(n3, "l_n3")
+        l_n4 = load_list(n4, "l_n4")
+        l_n5 = load_list(n5, "l_n5")
+        l_n1 = load_list(n1, "l_n1")
+        l_n2 = load_list(n2, "l_n2")
+        tab_w = windows("tab")
+        tab_rows = tab.rearrange("(p t) j -> p t j", t=PACK)
+        for t in range(PACK):
+            nc.sync.dma_start(tab_w[t][:], tab_rows[:, t, :])
+        w2_w = sbuf([P, 2 * S], U8, "w2_w")
+        nc.sync.dma_start(w2_w[:].bitcast(I32), w2_words[0].bitcast(I32))
+        load_scale_rows(nc.sync, w2_sc, w2_scales)
+        gn_sb = sbuf([P, PACK], F32, "gn_sb")
+        nc.sync.dma_start(gn_sb[:], gn.rearrange("(p t) o -> p (t o)", t=PACK))
+        l_n7 = load_list(n7, "l_n7")
+        l_n6 = load_list(n6, "l_n6")
+
+        xo_sc = sbuf([P, S], U8, "xo_sc")
+        xc_sc = sbuf([P, S], U8, "xc_sc")
+        xo_w = sbuf([P, S], I32, "xo_w")
+        xc_w = sbuf([P, S], I32, "xc_w")
+        xc_sc_d = sbuf([P, S], U8, "xc_sc_d")
+        xc_w_d = sbuf([P, S], I32, "xc_w_d")
+        w1_w_d = sbuf([P, 2 * S], U8, "w1_w_d")
+        w1_sc_d = sbuf([P, S], U8, "w1_sc_d")
+
+        def deal_fp4(dst, src):
+            nc.scalar.copy(
+                dst[:].bitcast(U16).rearrange("p (t b i) -> p b t i", t=PACK, i=8),
+                src[:].bitcast(U16).rearrange("p (b i t) -> p b t i", t=PACK, i=8),
+            )
+
+        def deal_weight_scales(dst, src):
+            nc.gpsimd.tensor_copy(
+                dst[:].rearrange("p (t m) -> p t m", t=PACK), src[:].rearrange("p (m t) -> p t m", t=PACK)
+            )
+
+        nc.vector.tensor_copy(xo_sc[:], x_sc[:].indirect(l_offs[:]))
+        nc.vector.tensor_copy(xc_sc[:], x_sc[:].indirect(l_cand[:]))
+        deal_fp4(w1_w_d, w1_w)
+        deal_weight_scales(w1_sc_d, w1_sc)
+        nc.vector.tensor_copy(xo_w[:].bitcast(U32), x_w[:].bitcast(U32).indirect(l_offs[:]))
+        gs34 = sbuf([P, PACK], F32, "gs34")
+        nc.gpsimd.tensor_scalar(gs34[:], gs_sb[:], 0.75, 0.0, ALU.mult, ALU.add)
+        nc.vector.tensor_copy(xc_w[:].bitcast(U32), x_w[:].bitcast(U32).indirect(l_cand[:]))
+        nc.vector.tensor_copy(
+            xc_sc_d[:].rearrange("p (t m) -> p m t", t=PACK), xc_sc[:].rearrange("p (m t) -> p m t", t=PACK)
+        )
+        nc.vector.tensor_copy(
+            xc_w_d[:].rearrange("p (t b i) -> p b t i", t=PACK, i=4),
+            xc_w[:].rearrange("p (b i t) -> p b t i", t=PACK, i=4),
+        )
+
+
+        def fetch(dst, t, h, window, lst):
+            nc.scalar.activation(dst[:, t, cols(h)], window[:].indirect(part(lst, h)), ACT.Copy)
+
+        def fp4(tile, t):
+            return tile[:, 2 * P * t : 2 * P * (t + 1)].bitcast(FP4X4)
+
+        def block(t):
+            return slice(P * t, P * (t + 1))
+
+        y = windows("y")
+        yg = windows("yg")
+        prod3 = planes("prod3", "left")
+        prod45 = planes("prod45", "right")
+        got4 = planes("got4")
+        for t in range(PACK):
+            acc = psum.tile([P, S], F32, name="y_acc%d" % t, tag="first%d" % t)
+            nc.tensor.matmul_mx(
+                acc[:], lhsT=fp4(w1_w_d, t), lhsT_scale=w1_sc_d[:, block(t)],
+                rhs=xo_w[:].bitcast(FP8X4), rhs_scale=xo_sc[:], start=True, stop=True,
+            )
+            nc.scalar.copy(y[t][:], acc[:])
+            nc.scalar.activation(yg[t][:], acc[:], ACT.Copy, scale=gs34[:, t : t + 1])
+            for h in range(HALVES):
+                nc.vector.tensor_tensor(prod3[:, t, cols(h)], y[t][:].indirect(part(l_n3, h)), yg[t][:, cols(h)], ALU.mult)
+                nc.scalar.activation(got4[:, t, cols(h)], yg[t][:].indirect(part(l_n4, h)), ACT.Copy)
+            for h in range(HALVES):
+                nc.vector.tensor_tensor(prod45[:, t, cols(h)], y[t][:].indirect(part(l_n5, h)), got4[:, t, cols(h)], ALU.mult)
+
+        def quantise(words, scales, woven, h):
+            nc.vector.quantize_mx(out=words[:, cols(h)].bitcast(FP8X4), scales=scales[:, cols(h)], in_=woven[:])
+
+        z2_w = sbuf([P, S], I32, "z2_w")
+        z2_sc = sbuf([P, S], U8, "z2_sc")
+        z2_bf = [sbuf([P, PACK * HALF], BF16, "z2_bf%d" % h) for h in range(HALVES)]
+        for h in range(HALVES):
+            nc.vector.tensor_tensor(
+                woven_by_pairs(z2_bf[h]), by_pairs(prod3[:, :, cols(h)]), by_pairs(prod45[:, :, cols(h)]), ALU.add
+            )
+        for h in range(HALVES):
+            quantise(z2_w, z2_sc, z2_bf[h], h)
+
+        w2_sc_d = sbuf([P, S], U8, "w2_sc_d", "yg1")
+        w2_w_d = sbuf([P, 2 * S], U8, "w2_w_d", "yg2")
+        nc.vector.tensor_copy(
+            w2_sc_d[:].rearrange("p (t m) -> p m t", t=PACK), w2_sc[:].rearrange("p (m t) -> p m t", t=PACK)
+        )
+        late = planes("late", "yg3")
+        for t in range(PACK):
+            for h in range(HALVES):
+                fetch(late, t, h, tab_w[t], l_n1)
+        deal_fp4(w2_w_d, w2_w)
+
+        b = windows("b")
+        b_acc = []
+        diff = planes("diff", "left")
+        size = planes("size", "right")
+        got7 = planes("got7")
+        for t in range(PACK):
+            acc = psum.tile([P, S], F32, name="b_acc%d" % t, tag="second%d" % t)
+            b_acc.append(acc)
+            nc.tensor.matmul_mx(
+                acc[:], lhsT=xc_w_d[:, block(t)].bitcast(FP8X4), lhsT_scale=xc_sc_d[:, block(t)],
+                rhs=z2_w[:].bitcast(FP8X4), rhs_scale=z2_sc[:], start=True, stop=True,
+            )
+
+        def make_diff(t):
+            for h in range(HALVES):
+                nc.vector.tensor_tensor(diff[:, t, cols(h)], y[t][:].indirect(part(l_n2, h)), late[:, t, cols(h)], ALU.add)
+            for h in range(HALVES):
+                nc.vector.tensor_tensor(diff[:, t, cols(h)], y[t][:, cols(h)], diff[:, t, cols(h)], ALU.subtract)
+
+        def make_size(t):
+            for h in range(HALVES):
+                nc.scalar.activation(size[:, t, cols(h)], diff[:, t, cols(h)], ACT.Abs)
+
+        def empty_b(t):
+            nc.scalar.activation(b[t][:], b_acc[t][:], ACT.Copy, scale=0.0625)
+
+        for t in range(PACK):
+            make_diff(t)
+        empty_b(0)
+        make_size(0)
+        make_size(1)
+        fetch(got7, 0, 0, b[0], l_n7)
+        empty_b(1)
+        make_size(2)
+        fetch(got7, 1, 0, b[1], l_n7)
+        empty_b(2)
+        make_size(3)
+        fetch(got7, 2, 0, b[2], l_n7)
+        empty_b(3)
+        fetch(got7, 3, 0, b[3], l_n7)
+
+        z_w = sbuf([P, S], I32, "z_w")
+        z_sc = sbuf([P, S], U8, "z_sc")
+        z_bf = [sbuf([P, PACK * HALF], BF16, "z_bf%d" % h) for h in range(HALVES)]
+        gn_wide = gn_sb[:].rearrange("p (c t i) -> p c t i", c=1, i=1).to_broadcast([P, HALF // 2, PACK, 2])
+        a = windows("a")
+        a_acc = {}
+        larger = planes("larger")
+        for h in range(HALVES):
+            nc.vector.tensor_tensor(woven_by_pairs(z_bf[h]), by_pairs(size[:, :, cols(h)]), gn_wide, ALU.mult)
+        for h in range(HALVES):
+            quantise(z_w, z_sc, z_bf[h], h)
+            for u in range(2):
+                acc = psum.tile([P, 2, HALF], F32, name="a_acc%d%d" % (h, u), tag="first%d" % (2 * h + u))
+                a_acc[h, u] = acc
+                for v in range(2):
+                    t = 2 * u + v
+                    nc.tensor.matmul_mx(
+                        acc[:, v, :], lhsT=fp4(w2_w_d, t), lhsT_scale=w2_sc_d[:, block(t)],
+                        rhs=z_w[:, cols(h)].bitcast(FP8X4), rhs_scale=z_sc[:, cols(h)], start=True, stop=True,
+                    )
+        for t in range(PACK):
+            fetch(got7, t, 1, b[t], l_n7)
+        for t in range(PACK):
+            nc.scalar.copy(a[t][:, cols(0)], a_acc[0, t // 2][:, t % 2, :])
+
+        def make_larger(h, u):
+            nc.vector.tensor_tensor(
+                larger[:, 2 * u : 2 * u + 2, cols(h)], a_acc[h, u][:], got7[:, 2 * u : 2 * u + 2, cols(h)], ALU.max
+            )
+
+        for u in range(2):
+            make_larger(0, u)
+
+        got6 = planes("got6")
+        result = planes("result")
+        o_w = sbuf([P, S], I32, "o_w")
+        o_sc = sbuf([P, S], U8, "o_sc")
+        o_bf = [sbuf([P, PACK * HALF], BF16, "o_bf%d" % h) for h in range(HALVES)]
+        out_rows = out_0.rearrange("(p t) j -> p t j", t=PACK)
+        out_words = out_1[0].rearrange("p n r -> p (n r)").bitcast(I32)
+        for h in range(HALVES):
+            for t in range(PACK):
+                if h == 0:
+                    nc.scalar.copy(a[t][:, cols(1)], a_acc[1, t // 2][:, t % 2, :])
+                fetch(got6, t, h, a[t], l_n6)
+                if h == 0 and t % 2 == 1:
+                    make_larger(1, t // 2)
+                nc.vector.scalar_tensor_tensor(
+                    got6[:, t, cols(h)], b_acc[t][:, cols(h)], 0.0625, got6[:, t, cols(h)], ALU.mult, ALU.min
+                )
+            for u in range(2):
+                two = slice(2 * u, 2 * u + 2)
+                nc.vector.tensor_tensor(result[:, two, cols(h)], larger[:, two, cols(h)], got6[:, two, cols(h)], ALU.subtract)
+                nc.sync.dma_start(out_rows[:, two, cols(h)], result[:, two, cols(h)])
+        nc.scalar.copy(woven_by_pairs(o_bf[0]), by_pairs(result[:, :, cols(0)]))
+        nc.vector.tensor_copy(woven_by_pairs(o_bf[1]), by_pairs(result[:, :, cols(1)]))
+        for h in range(HALVES):
+            quantise(o_w, o_sc, o_bf[h], h)
+            nc.sync.dma_start(out_words[:, cols(h)], o_w[:, cols(h)])
+        for q in range(4):
+            queue = nc.scalar if q % 2 == 0 else nc.sync
+            queue.dma_start(out_2[0, 4 * q : 4 * q + 4, :].bitcast(I32), o_sc[32 * q : 32 * q + 4, :].bitcast(I32))

@@ -20,6 +20,11 @@ P = 128
 PACK = 4
 HALF = S // 2
 HALVES = 2
+EARLY = []
+ON_VECTOR = []
+SCALED_ON_VECTOR = [0]
+UNFUSED = [3]
+SPARE = 16
 
 
 def tile_picked_fkcdmaxbkindddot_none_po_kernel(
@@ -55,13 +60,22 @@ def tile_picked_fkcdmaxbkindddot_none_po_kernel(
             return sbuf([P, PACK, S], F32, name, tag)
 
         def windows(name):
-            return [sbuf([P, S], F32, name + str(t)) for t in range(PACK)]
+            return [sbuf([P, S + SPARE], F32, name + str(t)) for t in range(PACK)]
 
         def by_pairs(ap):
             return ap.rearrange("p t (c i) -> p c t i", i=2)
 
         def woven_by_pairs(tile):
-            return tile[:].rearrange("p (c i t) -> p c t i", i=2, t=PACK)
+            return tile.rearrange("p (c i t) -> p c t i", i=2, t=PACK)
+
+        def span(first, count):
+            return slice(first, first + count)
+
+        def entries(lst, first, count):
+            return lst[:, first // 16 : (first + count) // 16]
+
+        whole = [(0, S)]
+        halves = [(0, HALF), (HALF, HALF)]
 
         x_sc = sbuf([P, T], U8, "x_sc")
         w1_sc = sbuf([P, S], U8, "w1_sc")
@@ -71,30 +85,41 @@ def tile_picked_fkcdmaxbkindddot_none_po_kernel(
         nc.gpsimd.memset(w1_sc[:].bitcast(I32), 0)
         nc.gpsimd.memset(w2_sc[:].bitcast(I32), 0)
 
+        tab_w = windows("tab")
+        y = windows("y")
+        yg = windows("yg")
+        b = planes("b")
+        a = planes("a")
+        for group in (tab_w, y, yg):
+            for tile in group:
+                nc.vector.memset(tile[:, S:], 0.0)
+
+        tab_rows = tab.rearrange("(p t) j -> p t j", t=PACK)
         l_offs = load_list(offs, "l_offs")
         l_cand = load_list(cand, "l_cand")
         load_scale_rows(nc.sync, x_sc, x_scales)
+        w1_w = sbuf([P, 2 * S], U8, "w1_w")
+        w2_w = sbuf([P, 2 * S], U8, "w2_w")
         x_w = sbuf([P, T], I32, "x_w")
         nc.sync.dma_start(x_w[:], x_words[0].rearrange("p n r -> p (n r)").bitcast(I32))
-        w1_w = sbuf([P, 2 * S], U8, "w1_w")
         nc.sync.dma_start(w1_w[:].bitcast(I32), w1_words[0].bitcast(I32))
         load_scale_rows(nc.sync, w1_sc, w1_scales)
         gs_sb = sbuf([P, PACK], F32, "gs_sb")
-        nc.sync.dma_start(gs_sb[:], gs.rearrange("(p t) o -> p (t o)", t=PACK))
+        nc.gpsimd.dma_start(gs_sb[:], gs.rearrange("(p t) o -> p (t o)", t=PACK))
+        gn_sb = sbuf([P, PACK], F32, "gn_sb")
+        nc.gpsimd.dma_start(gn_sb[:], gn.rearrange("(p t) o -> p (t o)", t=PACK))
+        l_n1 = load_list(n1, "l_n1")
+        nc.sync.dma_start(w2_w[:].bitcast(I32), w2_words[0].bitcast(I32))
+        for t in EARLY:
+            nc.sync.dma_start(tab_w[t][:, :S], tab_rows[:, t, :])
         l_n3 = load_list(n3, "l_n3")
         l_n4 = load_list(n4, "l_n4")
         l_n5 = load_list(n5, "l_n5")
-        l_n1 = load_list(n1, "l_n1")
         l_n2 = load_list(n2, "l_n2")
-        tab_w = windows("tab")
-        tab_rows = tab.rearrange("(p t) j -> p t j", t=PACK)
         for t in range(PACK):
-            nc.sync.dma_start(tab_w[t][:], tab_rows[:, t, :])
-        w2_w = sbuf([P, 2 * S], U8, "w2_w")
-        nc.sync.dma_start(w2_w[:].bitcast(I32), w2_words[0].bitcast(I32))
+            if t not in EARLY:
+                nc.sync.dma_start(tab_w[t][:, :S], tab_rows[:, t, :])
         load_scale_rows(nc.sync, w2_sc, w2_scales)
-        gn_sb = sbuf([P, PACK], F32, "gn_sb")
-        nc.sync.dma_start(gn_sb[:], gn.rearrange("(p t) o -> p (t o)", t=PACK))
         l_n7 = load_list(n7, "l_n7")
         l_n6 = load_list(n6, "l_n6")
 
@@ -102,7 +127,6 @@ def tile_picked_fkcdmaxbkindddot_none_po_kernel(
         xc_sc = sbuf([P, S], U8, "xc_sc")
         xo_w = sbuf([P, S], I32, "xo_w")
         xc_w = sbuf([P, S], I32, "xc_w")
-        xc_sc_d = sbuf([P, S], U8, "xc_sc_d")
         xc_w_d = sbuf([P, S], I32, "xc_w_d")
         w1_w_d = sbuf([P, 2 * S], U8, "w1_w_d")
         w1_sc_d = sbuf([P, S], U8, "w1_sc_d")
@@ -113,30 +137,42 @@ def tile_picked_fkcdmaxbkindddot_none_po_kernel(
                 src[:].bitcast(U16).rearrange("p (b i t) -> p b t i", t=PACK, i=8),
             )
 
-        def deal_weight_scales(dst, src):
-            nc.gpsimd.tensor_copy(
-                dst[:].rearrange("p (t m) -> p t m", t=PACK), src[:].rearrange("p (m t) -> p t m", t=PACK)
+        def deal_bytes(dst, src):
+            nc.vector.tensor_copy(
+                dst[:].rearrange("p (t m) -> p m t", t=PACK), src[:].rearrange("p (m t) -> p m t", t=PACK)
             )
+
+        def fetch(dst, t, piece, window, lst):
+            nc.scalar.activation(dst[:, t, span(*piece)], window[:].indirect(entries(lst, *piece)), ACT.Copy)
+
+        def fetch_with(dst, t, piece, window, lst, other, op):
+            nc.vector.tensor_tensor(dst[:, t, span(*piece)], window[:].indirect(entries(lst, *piece)), other[:, span(*piece)], op)
 
         nc.vector.tensor_copy(xo_sc[:], x_sc[:].indirect(l_offs[:]))
         nc.vector.tensor_copy(xc_sc[:], x_sc[:].indirect(l_cand[:]))
         deal_fp4(w1_w_d, w1_w)
-        deal_weight_scales(w1_sc_d, w1_sc)
-        nc.vector.tensor_copy(xo_w[:].bitcast(U32), x_w[:].bitcast(U32).indirect(l_offs[:]))
         gs34 = sbuf([P, PACK], F32, "gs34")
         nc.gpsimd.tensor_scalar(gs34[:], gs_sb[:], 0.75, 0.0, ALU.mult, ALU.add)
+        for some in (slice(0, 1), slice(1, PACK)):
+            nc.gpsimd.tensor_copy(
+                w1_sc_d[:].rearrange("p (t m) -> p t m", t=PACK)[:, some, :],
+                w1_sc[:].rearrange("p (m t) -> p t m", t=PACK)[:, some, :],
+            )
+        for piece in halves:
+            nc.vector.tensor_copy(xo_w[:, span(*piece)].bitcast(U32), x_w[:].bitcast(U32).indirect(entries(l_offs, *piece)))
         nc.vector.tensor_copy(xc_w[:].bitcast(U32), x_w[:].bitcast(U32).indirect(l_cand[:]))
-        nc.vector.tensor_copy(
-            xc_sc_d[:].rearrange("p (t m) -> p m t", t=PACK), xc_sc[:].rearrange("p (m t) -> p m t", t=PACK)
-        )
+        xc_sc_d = sbuf([P, S], U8, "xc_sc_d", "x_w")
+        deal_bytes(xc_sc_d, xc_sc)
         nc.vector.tensor_copy(
             xc_w_d[:].rearrange("p (t b i) -> p b t i", t=PACK, i=4),
             xc_w[:].rearrange("p (b i t) -> p b t i", t=PACK, i=4),
         )
-
-
-        def fetch(dst, t, h, window, lst):
-            nc.scalar.activation(dst[:, t, cols(h)], window[:].indirect(part(lst, h)), ACT.Copy)
+        w2_w_d = sbuf([P, 2 * S], U8, "w2_w_d")
+        deal_fp4(w2_w_d, w2_w)
+        early = planes("early")
+        for t in EARLY:
+            for piece in halves:
+                fetch(early, t, piece, tab_w[t], l_n1)
 
         def fp4(tile, t):
             return tile[:, 2 * P * t : 2 * P * (t + 1)].bitcast(FP4X4)
@@ -144,122 +180,170 @@ def tile_picked_fkcdmaxbkindddot_none_po_kernel(
         def block(t):
             return slice(P * t, P * (t + 1))
 
-        y = windows("y")
-        yg = windows("yg")
         prod3 = planes("prod3", "left")
         prod45 = planes("prod45", "right")
         got4 = planes("got4")
-        for t in range(PACK):
+
+        def make_y(t):
             acc = psum.tile([P, S], F32, name="y_acc%d" % t, tag="first%d" % t)
-            nc.tensor.matmul_mx(
-                acc[:], lhsT=fp4(w1_w_d, t), lhsT_scale=w1_sc_d[:, block(t)],
-                rhs=xo_w[:].bitcast(FP8X4), rhs_scale=xo_sc[:], start=True, stop=True,
-            )
-            nc.scalar.copy(y[t][:], acc[:])
-            nc.scalar.activation(yg[t][:], acc[:], ACT.Copy, scale=gs34[:, t : t + 1])
-            for h in range(HALVES):
-                nc.vector.tensor_tensor(prod3[:, t, cols(h)], y[t][:].indirect(part(l_n3, h)), yg[t][:, cols(h)], ALU.mult)
-                nc.scalar.activation(got4[:, t, cols(h)], yg[t][:].indirect(part(l_n4, h)), ACT.Copy)
-            for h in range(HALVES):
-                nc.vector.tensor_tensor(prod45[:, t, cols(h)], y[t][:].indirect(part(l_n5, h)), got4[:, t, cols(h)], ALU.mult)
+            for piece in halves if t == 0 else [(0, S)]:
+                at = span(*piece)
+                nc.tensor.matmul_mx(
+                    acc[:, at], lhsT=fp4(w1_w_d, t), lhsT_scale=w1_sc_d[:, block(t)],
+                    rhs=xo_w[:, at].bitcast(FP8X4), rhs_scale=xo_sc[:, at], start=True, stop=True,
+                )
+            nc.scalar.copy(y[t][:, :S], acc[:])
+            if t in SCALED_ON_VECTOR:
+                nc.vector.tensor_scalar(yg[t][:, :S], y[t][:, :S], gs34[:, t : t + 1], None, ALU.mult)
+            else:
+                nc.scalar.activation(yg[t][:, :S], acc[:], ACT.Copy, scale=gs34[:, t : t + 1])
+
+        def multiply(t, pieces):
+            for piece in whole:
+                fetch_with(prod3, t, piece, y[t], l_n3, yg[t], ALU.mult)
+            for piece in pieces:
+                fetch(got4, t, piece, yg[t], l_n4)
+            for piece in pieces:
+                fetch_with(prod45, t, piece, y[t], l_n5, got4[:, t, :], ALU.mult)
+
+        make_y(0)
+        multiply(0, halves)
+        make_y(1)
+        multiply(1, whole)
+        make_y(2)
+        make_y(3)
+        multiply(2, whole)
+        multiply(3, halves)
 
         def quantise(words, scales, woven, h):
             nc.vector.quantize_mx(out=words[:, cols(h)].bitcast(FP8X4), scales=scales[:, cols(h)], in_=woven[:])
 
+        def product(acc, h, lhsT, lhsT_scale, words, scales):
+            nc.tensor.matmul_mx(
+                acc, lhsT=lhsT, lhsT_scale=lhsT_scale, rhs=words[:, cols(h)].bitcast(FP8X4),
+                rhs_scale=scales[:, cols(h)], start=True, stop=True,
+            )
+
         z2_w = sbuf([P, S], I32, "z2_w")
         z2_sc = sbuf([P, S], U8, "z2_sc")
         z2_bf = [sbuf([P, PACK * HALF], BF16, "z2_bf%d" % h) for h in range(HALVES)]
-        for h in range(HALVES):
-            nc.vector.tensor_tensor(
-                woven_by_pairs(z2_bf[h]), by_pairs(prod3[:, :, cols(h)]), by_pairs(prod45[:, :, cols(h)]), ALU.add
-            )
-        for h in range(HALVES):
-            quantise(z2_w, z2_sc, z2_bf[h], h)
+        b_acc = {}
 
-        w2_sc_d = sbuf([P, S], U8, "w2_sc_d", "yg1")
-        w2_w_d = sbuf([P, 2 * S], U8, "w2_w_d", "yg2")
-        nc.vector.tensor_copy(
-            w2_sc_d[:].rearrange("p (t m) -> p m t", t=PACK), w2_sc[:].rearrange("p (m t) -> p m t", t=PACK)
-        )
+        def add_products(h, first, count):
+            at = span(h * HALF + first, count)
+            nc.vector.tensor_tensor(
+                woven_by_pairs(z2_bf[h][:, span(PACK * first, PACK * count)]),
+                by_pairs(prod3[:, :, at]), by_pairs(prod45[:, :, at]), ALU.add,
+            )
+
+        def make_b(h):
+            quantise(z2_w, z2_sc, z2_bf[h], h)
+            for u in range(2):
+                b_acc[h, u] = psum.tile([P, 2, HALF], F32, name="b_acc%d%d" % (h, u), tag="second%d" % (2 * h + u))
+                for v in range(2):
+                    t = 2 * u + v
+                    product(b_acc[h, u][:, v, :], h, xc_w_d[:, block(t)].bitcast(FP8X4), xc_sc_d[:, block(t)], z2_w, z2_sc)
+
+        add_products(0, 0, HALF)
+        make_b(0)
+        add_products(1, 0, HALF // 2)
+        add_products(1, HALF // 2, HALF // 2)
+        make_b(1)
+
+        w2_sc_d = sbuf([P, S], U8, "w2_sc_d", "z2_bf0")
+        deal_bytes(w2_sc_d, w2_sc)
         late = planes("late", "yg3")
         for t in range(PACK):
-            for h in range(HALVES):
-                fetch(late, t, h, tab_w[t], l_n1)
-        deal_fp4(w2_w_d, w2_w)
+            for piece in whole:
+                if t not in EARLY:
+                    fetch(late, t, piece, tab_w[t], l_n1)
 
-        b = windows("b")
-        b_acc = []
+        got2 = planes("got2", "got4")
+        for t in UNFUSED:
+            for piece in whole:
+                fetch(got2, t, piece, y[t], l_n2)
         diff = planes("diff", "left")
         size = planes("size", "right")
         got7 = planes("got7")
-        for t in range(PACK):
-            acc = psum.tile([P, S], F32, name="b_acc%d" % t, tag="second%d" % t)
-            b_acc.append(acc)
-            nc.tensor.matmul_mx(
-                acc[:], lhsT=xc_w_d[:, block(t)].bitcast(FP8X4), lhsT_scale=xc_sc_d[:, block(t)],
-                rhs=z2_w[:].bitcast(FP8X4), rhs_scale=z2_sc[:], start=True, stop=True,
-            )
 
-        def make_diff(t):
-            for h in range(HALVES):
-                nc.vector.tensor_tensor(diff[:, t, cols(h)], y[t][:].indirect(part(l_n2, h)), late[:, t, cols(h)], ALU.add)
-            for h in range(HALVES):
-                nc.vector.tensor_tensor(diff[:, t, cols(h)], y[t][:, cols(h)], diff[:, t, cols(h)], ALU.subtract)
+        def make_diff(t, pieces):
+            kinds = early if t in EARLY else late
+            for piece in pieces:
+                if t in UNFUSED:
+                    nc.vector.tensor_tensor(diff[:, t, span(*piece)], late[:, t, span(*piece)], got2[:, t, span(*piece)], ALU.add)
+                else:
+                    fetch_with(diff, t, piece, y[t], l_n2, kinds[:, t, :], ALU.add)
+            for piece in pieces:
+                at = span(*piece)
+                nc.vector.tensor_tensor(diff[:, t, at], y[t][:, at], diff[:, t, at], ALU.subtract)
 
-        def make_size(t):
-            for h in range(HALVES):
-                nc.scalar.activation(size[:, t, cols(h)], diff[:, t, cols(h)], ACT.Abs)
+        def make_size(t, pieces):
+            for piece in pieces:
+                nc.scalar.activation(size[:, t, span(*piece)], diff[:, t, span(*piece)], ACT.Abs)
 
-        def empty_b(t):
-            nc.scalar.activation(b[t][:], b_acc[t][:], ACT.Copy, scale=0.0625)
+        def empty_b(h, u):
+            nc.scalar.activation(b[:, 2 * u : 2 * u + 2, cols(h)], b_acc[h, u][:], ACT.Copy, scale=0.0625)
 
-        for t in range(PACK):
-            make_diff(t)
-        empty_b(0)
-        make_size(0)
-        make_size(1)
-        fetch(got7, 0, 0, b[0], l_n7)
-        empty_b(1)
-        make_size(2)
-        fetch(got7, 1, 0, b[1], l_n7)
-        empty_b(2)
-        make_size(3)
-        fetch(got7, 2, 0, b[2], l_n7)
-        empty_b(3)
-        fetch(got7, 3, 0, b[3], l_n7)
+        def fetch_b(t, pieces):
+            for piece in pieces:
+                fetch(got7_held if t in [0,1,2] else got7, t, piece, b[:, t, :], l_n7)
+
+        make_diff(0, whole)
+        make_diff(1, whole)
+        for h in range(HALVES):
+            make_diff(2, halves[h : h + 1])
+            make_diff(3, halves[h : h + 1])
+        empty_b(0, 0)
+        empty_b(0, 1)
+        empty_b(1, 0)
+        make_size(0, whole)
+        make_size(1, whole)
+        empty_b(1, 1)
+        for h in range(HALVES):
+            make_size(2, halves[h : h + 1])
+            make_size(3, halves[h : h + 1])
+        got7_held = planes("got7_held", "left")
+        fetch_b(0, halves)
+        fetch_b(1, halves)
+        for h in range(HALVES):
+            for t in (2, 3):
+                if [t, h] not in [[3,0],[3,1]]:
+                    fetch_b(t, halves[h : h + 1])
 
         z_w = sbuf([P, S], I32, "z_w")
         z_sc = sbuf([P, S], U8, "z_sc")
         z_bf = [sbuf([P, PACK * HALF], BF16, "z_bf%d" % h) for h in range(HALVES)]
-        gn_wide = gn_sb[:].rearrange("p (c t i) -> p c t i", c=1, i=1).to_broadcast([P, HALF // 2, PACK, 2])
-        a = windows("a")
         a_acc = {}
         larger = planes("larger")
-        for h in range(HALVES):
-            nc.vector.tensor_tensor(woven_by_pairs(z_bf[h]), by_pairs(size[:, :, cols(h)]), gn_wide, ALU.mult)
-        for h in range(HALVES):
-            quantise(z_w, z_sc, z_bf[h], h)
-            for u in range(2):
-                acc = psum.tile([P, 2, HALF], F32, name="a_acc%d%d" % (h, u), tag="first%d" % (2 * h + u))
-                a_acc[h, u] = acc
-                for v in range(2):
-                    t = 2 * u + v
-                    nc.tensor.matmul_mx(
-                        acc[:, v, :], lhsT=fp4(w2_w_d, t), lhsT_scale=w2_sc_d[:, block(t)],
-                        rhs=z_w[:, cols(h)].bitcast(FP8X4), rhs_scale=z_sc[:, cols(h)], start=True, stop=True,
-                    )
-        for t in range(PACK):
-            fetch(got7, t, 1, b[t], l_n7)
-        for t in range(PACK):
-            nc.scalar.copy(a[t][:, cols(0)], a_acc[0, t // 2][:, t % 2, :])
 
-        def make_larger(h, u):
+        def scale_size(h, first, count):
+            gn_wide = gn_sb[:].rearrange("p (c t i) -> p c t i", c=1, i=1).to_broadcast([P, count // 2, PACK, 2])
             nc.vector.tensor_tensor(
-                larger[:, 2 * u : 2 * u + 2, cols(h)], a_acc[h, u][:], got7[:, 2 * u : 2 * u + 2, cols(h)], ALU.max
+                woven_by_pairs(z_bf[h][:, span(PACK * first, PACK * count)]),
+                by_pairs(size[:, :, span(h * HALF + first, count)]), gn_wide, ALU.mult,
             )
 
-        for u in range(2):
-            make_larger(0, u)
+        for h in range(HALVES):
+            scale_size(h, 0, HALF)
+        for h in range(HALVES):
+            quantise(z_w, z_sc, z_bf[h], h)
+        got7_late = planes("got7_late", "right")
+        for t, h in [[3,0],[3,1]]:
+            nc.vector.tensor_copy(got7_late[:, t, cols(h)], b[:, t, :].indirect(part(l_n7, h)))
+        for t in range(PACK):
+            a_acc[t] = psum.tile([P, S], F32, name="a_acc%d" % t, tag="first%d" % t)
+            nc.tensor.matmul_mx(
+                a_acc[t][:], lhsT=fp4(w2_w_d, t), lhsT_scale=w2_sc_d[:, block(t)],
+                rhs=z_w[:].bitcast(FP8X4), rhs_scale=z_sc[:], start=True, stop=True,
+            )
+
+        def make_larger(t):
+            where = [got7_late if [t, h] in [[3,0],[3,1]] else got7_held if t in [0,1,2] else got7 for h in range(HALVES)]
+            if where[0] is where[1]:
+                nc.vector.tensor_tensor(larger[:, t, :], a_acc[t][:], where[0][:, t, :], ALU.max)
+            else:
+                for h in range(HALVES):
+                    nc.vector.tensor_tensor(larger[:, t, cols(h)], a_acc[t][:, cols(h)], where[h][:, t, cols(h)], ALU.max)
 
         got6 = planes("got6")
         result = planes("result")
@@ -268,22 +352,49 @@ def tile_picked_fkcdmaxbkindddot_none_po_kernel(
         o_bf = [sbuf([P, PACK * HALF], BF16, "o_bf%d" % h) for h in range(HALVES)]
         out_rows = out_0.rearrange("(p t) j -> p t j", t=PACK)
         out_words = out_1[0].rearrange("p n r -> p (n r)").bitcast(I32)
-        for h in range(HALVES):
-            for t in range(PACK):
-                if h == 0:
-                    nc.scalar.copy(a[t][:, cols(1)], a_acc[1, t // 2][:, t % 2, :])
-                fetch(got6, t, h, a[t], l_n6)
-                if h == 0 and t % 2 == 1:
-                    make_larger(1, t // 2)
-                nc.vector.scalar_tensor_tensor(
-                    got6[:, t, cols(h)], b_acc[t][:, cols(h)], 0.0625, got6[:, t, cols(h)], ALU.mult, ALU.min
-                )
-            for u in range(2):
-                two = slice(2 * u, 2 * u + 2)
-                nc.vector.tensor_tensor(result[:, two, cols(h)], larger[:, two, cols(h)], got6[:, two, cols(h)], ALU.subtract)
-                nc.sync.dma_start(out_rows[:, two, cols(h)], result[:, two, cols(h)])
-        nc.scalar.copy(woven_by_pairs(o_bf[0]), by_pairs(result[:, :, cols(0)]))
-        nc.vector.tensor_copy(woven_by_pairs(o_bf[1]), by_pairs(result[:, :, cols(1)]))
+
+        def fetch_a(t, h):
+            if [t, h] in ON_VECTOR:
+                nc.vector.tensor_copy(got6[:, t, cols(h)], a[:, t, :].indirect(part(l_n6, h)))
+            else:
+                fetch(got6, t, halves[h], a[:, t, :], l_n6)
+
+        def empty_a(t):
+            empty = nc.vector.tensor_copy if t in [0,2] else nc.scalar.copy
+            empty(a[:, t, :], a_acc[t][:])
+
+        def finish(h, first, count, engine):
+            some = span(first, count)
+            nc.vector.scalar_tensor_tensor(
+                got6[:, some, cols(h)], b_acc[h, first // 2][:, span(first % 2, count), :], 0.0625,
+                got6[:, some, cols(h)], ALU.mult, ALU.min,
+            )
+            engine.tensor_tensor(result[:, some, cols(h)], larger[:, some, cols(h)], got6[:, some, cols(h)], ALU.subtract)
+
+        empty_a(0)
+        empty_a(1)
+        make_larger(0)
+        fetch_a(0, 0)
+        empty_a(2)
+        make_larger(1)
+        fetch_a(1, 0)
+        empty_a(3)
+        make_larger(2)
+        fetch_a(2, 0)
+        make_larger(3)
+        fetch_a(3, 0)
+        finish(0, 0, 2, nc.vector)
+        finish(0, 2, 2, nc.vector)
+        nc.sync.dma_start(out_rows[:, :, cols(0)], result[:, :, cols(0)])
+        for t in range(PACK):
+            fetch_a(t, 1)
+        finish(1, 0, 2, nc.vector)
+        nc.sync.dma_start(out_rows[:, :2, cols(1)], result[:, :2, cols(1)])
+        finish(1, 2, 1, nc.vector)
+        finish(1, 3, 1, nc.vector)
+        nc.sync.dma_start(out_rows[:, 2:, cols(1)], result[:, 2:, cols(1)])
+        nc.scalar.copy(woven_by_pairs(o_bf[0][:]), by_pairs(result[:, :, cols(0)]))
+        nc.vector.tensor_copy(woven_by_pairs(o_bf[1][:]), by_pairs(result[:, :, cols(1)]))
         for h in range(HALVES):
             quantise(o_w, o_sc, o_bf[h], h)
             nc.sync.dma_start(out_words[:, cols(h)], o_w[:, cols(h)])

@@ -63,10 +63,10 @@ def tile_picked_fkcdmaxbkindddot_none_po_kernel(
             return [sbuf([P, S + SPARE], F32, name + str(t)) for t in range(PACK)]
 
         def by_pairs(ap):
-            return ap.rearrange("p t (c i) -> p c t i", i=2)
+            return ap.rearrange("p t (c i) -> p c t i", i=4)
 
         def woven_by_pairs(tile):
-            return tile.rearrange("p (c i t) -> p c t i", i=2, t=PACK)
+            return tile.rearrange("p (c i t) -> p c t i", i=4, t=PACK)
 
         def span(first, count):
             return slice(first, first + count)
@@ -139,7 +139,7 @@ def tile_picked_fkcdmaxbkindddot_none_po_kernel(
 
         def deal_bytes(dst, src):
             nc.vector.tensor_copy(
-                dst[:].rearrange("p (t m) -> p m t", t=PACK), src[:].rearrange("p (m t) -> p m t", t=PACK)
+                dst[:].rearrange("p (t b i) -> p b t i", t=PACK, i=16), src[:].rearrange("p (b i t) -> p b t i", t=PACK, i=16)
             )
 
         def fetch(dst, t, piece, window, lst):
@@ -317,7 +317,7 @@ def tile_picked_fkcdmaxbkindddot_none_po_kernel(
         larger = planes("larger")
 
         def scale_size(h, first, count):
-            gn_wide = gn_sb[:].rearrange("p (c t i) -> p c t i", c=1, i=1).to_broadcast([P, count // 2, PACK, 2])
+            gn_wide = gn_sb[:].rearrange("p (c t i) -> p c t i", c=1, i=1).to_broadcast([P, count // 4, PACK, 4])
             nc.vector.tensor_tensor(
                 woven_by_pairs(z_bf[h][:, span(PACK * first, PACK * count)]),
                 by_pairs(size[:, :, span(h * HALF + first, count)]), gn_wide, ALU.mult,

from contextlib import ExitStack

import concourse.mybir as mybir

K, T, S = 512, 2048, 512
FLOPS = 3 * 2 * 512 * 512 * 512

F32 = mybir.dt.float32
BF16 = mybir.dt.bfloat16
I32 = mybir.dt.int32
U32 = mybir.dt.uint32
U16 = mybir.dt.uint16
U8 = mybir.dt.uint8
FP8X4 = mybir.dt.float8_e4m3fn_x4
FP4X4 = mybir.dt.float4_e2m1fn_x4
ALU = mybir.AluOpType
ACT = mybir.ActivationFunctionType

P = 128
PACK = 4
HALF = S // 2
HALVES = 2
EARLY = []
ON_VECTOR = []
SCALED_ON_VECTOR = [0]
UNFUSED = [3]
SPARE = 16


def tile_picked_fkcdmaxbkindddot_none_po_kernel(
    tc, x_words, x_scales, w1_words, w1_scales, tab, gn, w2_words, w2_scales, gs,
    offs, n1, n2, n3, n4, n5, cand, n6, n7, out_0, out_1, out_2,
):
    nc = tc.nc

    with ExitStack() as ctx:
        lists = ctx.enter_context(tc.tile_pool(name="lists", bufs=1))
        keep = ctx.enter_context(tc.tile_pool(name="keep", bufs=1))
        psum = ctx.enter_context(tc.psum_pool(name="psum", bufs=1))

        def cols(h):
            return slice(h * HALF, (h + 1) * HALF)

        def load_list(src, name):
            tile = lists.tile([P, S // 16], U16, name=name)
            nc.sync.dma_start(tile[:], src)
            return tile

        def part(lst, h):
            return lst[:, h * HALF // 16 : (h + 1) * HALF // 16]

        def load_scale_rows(queue, tile, src):
            for q in range(4):
                queue.dma_start(tile[32 * q : 32 * q + 4, :].bitcast(I32), src[0, 4 * q : 4 * q + 4, :].bitcast(I32))

        def sbuf(shape, dtype, name, tag=None):
            return keep.tile(shape, dtype, name=name, tag=tag or name, align_bytes=64)

        def planes(name, tag=None):
            return sbuf([P, PACK, S], F32, name, tag)

        def windows(name):
            return [sbuf([P, S + SPARE], F32, name + str(t)) for t in range(PACK)]

        def by_pairs(ap):
            return ap.rearrange("p t (c i) -> p c t i", i=4)

        def woven_by_pairs(tile):
            return tile.rearrange("p (c i t) -> p c t i", i=4, t=PACK)

        def span(first, count):
            return slice(first, first + count)

        def entries(lst, first, count):
            return lst[:, first // 16 : (first + count) // 16]

        whole = [(0, S)]
        halves = [(0, HALF), (HALF, HALF)]

        x_sc = sbuf([P, T], U8, "x_sc")
        w1_sc = sbuf([P, S], U8, "w1_sc")
        w2_sc = sbuf([P, S], U8, "w2_sc")
        nc.vector.memset(x_sc[:, : T // 2].bitcast(I32), 0)
        nc.gpsimd.memset(x_sc[:, T // 2 :].bitcast(I32), 0)
        nc.gpsimd.memset(w1_sc[:].bitcast(I32), 0)
        nc.gpsimd.memset(w2_sc[:].bitcast(I32), 0)

        tab_w = windows("tab")
        y = windows("y")
        yg = windows("yg")
        b = planes("b")
        a = planes("a")
        for group in (tab_w, y, yg):
            for tile in group:
                nc.vector.memset(tile[:, S:], 0.0)

        tab_rows = tab.rearrange("(p t) j -> p t j", t=PACK)
        l_offs = load_list(offs, "l_offs")
        l_cand = load_list(cand, "l_cand")
        load_scale_rows(nc.sync, x_sc, x_scales)
        w1_w = sbuf([P, 2 * S], U8, "w1_w")
        w2_w = sbuf([P, 2 * S], U8, "w2_w")
        x_w = sbuf([P, T], I32, "x_w")
        nc.sync.dma_start(x_w[:], x_words[0].rearrange("p n r -> p (n r)").bitcast(I32))
        nc.sync.dma_start(w1_w[:].bitcast(I32), w1_words[0].bitcast(I32))
        load_scale_rows(nc.sync, w1_sc, w1_scales)
        gs_sb = sbuf([P, PACK], F32, "gs_sb")
        nc.gpsimd.dma_start(gs_sb[:], gs.rearrange("(p t) o -> p (t o)", t=PACK))
        gn_sb = sbuf([P, PACK], F32, "gn_sb")
        nc.gpsimd.dma_start(gn_sb[:], gn.rearrange("(p t) o -> p (t o)", t=PACK))
        l_n1 = load_list(n1, "l_n1")
        nc.sync.dma_start(w2_w[:].bitcast(I32), w2_words[0].bitcast(I32))
        for t in EARLY:
            nc.sync.dma_start(tab_w[t][:, :S], tab_rows[:, t, :])
        l_n3 = load_list(n3, "l_n3")
        l_n4 = load_list(n4, "l_n4")
        l_n5 = load_list(n5, "l_n5")
        l_n2 = load_list(n2, "l_n2")
        for t in range(PACK):
            if t not in EARLY:
                nc.sync.dma_start(tab_w[t][:, :S], tab_rows[:, t, :])
        load_scale_rows(nc.sync, w2_sc, w2_scales)
        l_n7 = load_list(n7, "l_n7")
        l_n6 = load_list(n6, "l_n6")

        xo_sc = sbuf([P, S], U8, "xo_sc")
        xc_sc = sbuf([P, S], U8, "xc_sc")
        xo_w = sbuf([P, S], I32, "xo_w")
        xc_w = sbuf([P, S], I32, "xc_w")
        xc_w_d = sbuf([P, S], I32, "xc_w_d")
        w1_w_d = sbuf([P, 2 * S], U8, "w1_w_d")
        w1_sc_d = sbuf([P, S], U8, "w1_sc_d")

        def deal_fp4(dst, src):
            nc.scalar.copy(
                dst[:].bitcast(U16).rearrange("p (t b i) -> p b t i", t=PACK, i=8),
                src[:].bitcast(U16).rearrange("p (b i t) -> p b t i", t=PACK, i=8),
            )

        def deal_bytes(dst, src):
            nc.vector.tensor_copy(
                dst[:].rearrange("p (t b i) -> p b t i", t=PACK, i=16), src[:].rearrange("p (b i t) -> p b t i", t=PACK, i=16)
            )

        def fetch(dst, t, piece, window, lst):
            nc.scalar.activation(dst[:, t, span(*piece)], window[:].indirect(entries(lst, *piece)), ACT.Copy)

        def fetch_with(dst, t, piece, window, lst, other, op):
            nc.vector.tensor_tensor(dst[:, t, span(*piece)], window[:].indirect(entries(lst, *piece)), other[:, span(*piece)], op)

        nc.vector.tensor_copy(xo_sc[:], x_sc[:].indirect(l_offs[:]))
        nc.vector.tensor_copy(xc_sc[:], x_sc[:].indirect(l_cand[:]))
        deal_fp4(w1_w_d, w1_w)
        gs34 = sbuf([P, PACK], F32, "gs34")
        nc.gpsimd.tensor_scalar(gs34[:], gs_sb[:], 0.75, 0.0, ALU.mult, ALU.add)
        for some in (slice(0, 1), slice(1, PACK)):
            nc.gpsimd.tensor_copy(
                w1_sc_d[:].rearrange("p (t m) -> p t m", t=PACK)[:, some, :],
                w1_sc[:].rearrange("p (m t) -> p t m", t=PACK)[:, some, :],
            )
        for piece in halves:
            nc.vector.tensor_copy(xo_w[:, span(*piece)].bitcast(U32), x_w[:].bitcast(U32).indirect(entries(l_offs, *piece)))
        nc.vector.tensor_copy(xc_w[:].bitcast(U32), x_w[:].bitcast(U32).indirect(l_cand[:]))
        xc_sc_d = sbuf([P, S], U8, "xc_sc_d", "x_w")
        deal_bytes(xc_sc_d, xc_sc)
        nc.vector.tensor_copy(
            xc_w_d[:].rearrange("p (t b i) -> p b t i", t=PACK, i=4),
            xc_w[:].rearrange("p (b i t) -> p b t i", t=PACK, i=4),
        )
        w2_w_d = sbuf([P, 2 * S], U8, "w2_w_d")
        deal_fp4(w2_w_d, w2_w)
        early = planes("early")
        for t in EARLY:
            for piece in halves:
                fetch(early, t, piece, tab_w[t], l_n1)

        def fp4(tile, t):
            return tile[:, 2 * P * t : 2 * P * (t + 1)].bitcast(FP4X4)

        def block(t):
            return slice(P * t, P * (t + 1))

        prod3 = planes("prod3", "left")
        prod45 = planes("prod45", "right")
        got4 = planes("got4")

        def make_y(t):
            acc = psum.tile([P, S], F32, name="y_acc%d" % t, tag="first%d" % t)
            for piece in halves if t == 0 else [(0, S)]:
                at = span(*piece)
                nc.tensor.matmul_mx(
                    acc[:, at], lhsT=fp4(w1_w_d, t), lhsT_scale=w1_sc_d[:, block(t)],
                    rhs=xo_w[:, at].bitcast(FP8X4), rhs_scale=xo_sc[:, at], start=True, stop=True,
                )
            nc.scalar.copy(y[t][:, :S], acc[:])
            if t in SCALED_ON_VECTOR:
                nc.vector.tensor_scalar(yg[t][:, :S], y[t][:, :S], gs34[:, t : t + 1], None, ALU.mult)
            else:
                nc.scalar.activation(yg[t][:, :S], acc[:], ACT.Copy, scale=gs34[:, t : t + 1])

        def multiply(t, pieces):
            for piece in whole:
                fetch_with(prod3, t, piece, y[t], l_n3, yg[t], ALU.mult)
            for piece in pieces:
                fetch(got4, t, piece, yg[t], l_n4)
            for piece in pieces:
                fetch_with(prod45, t, piece, y[t], l_n5, got4[:, t, :], ALU.mult)

        make_y(0)
        multiply(0, halves)
        make_y(1)
        multiply(1, whole)
        make_y(2)
        make_y(3)
        multiply(2, whole)
        multiply(3, halves)

        def quantise(words, scales, woven, h):
            nc.vector.quantize_mx(out=words[:, cols(h)].bitcast(FP8X4), scales=scales[:, cols(h)], in_=woven[:])

        def product(acc, h, lhsT, lhsT_scale, words, scales):
            nc.tensor.matmul_mx(
                acc, lhsT=lhsT, lhsT_scale=lhsT_scale, rhs=words[:, cols(h)].bitcast(FP8X4),
                rhs_scale=scales[:, cols(h)], start=True, stop=True,
            )

        z2_w = sbuf([P, S], I32, "z2_w")
        z2_sc = sbuf([P, S], U8, "z2_sc")
        z2_bf = [sbuf([P, PACK * HALF], BF16, "z2_bf%d" % h) for h in range(HALVES)]
        b_acc = {}

        def add_products(h, first, count):
            at = span(h * HALF + first, count)
            nc.vector.tensor_tensor(
                woven_by_pairs(z2_bf[h][:, span(PACK * first, PACK * count)]),
                by_pairs(prod3[:, :, at]), by_pairs(prod45[:, :, at]), ALU.add,
            )

        def make_b(h):
            quantise(z2_w, z2_sc, z2_bf[h], h)
            for u in range(2):
                b_acc[h, u] = psum.tile([P, 2, HALF], F32, name="b_acc%d%d" % (h, u), tag="second%d" % (2 * h + u))
                for v in range(2):
                    t = 2 * u + v
                    product(b_acc[h, u][:, v, :], h, xc_w_d[:, block(t)].bitcast(FP8X4), xc_sc_d[:, block(t)], z2_w, z2_sc)

        add_products(0, 0, HALF)
        make_b(0)
        add_products(1, 0, HALF // 2)
        add_products(1, HALF // 2, HALF // 2)
        make_b(1)

        w2_sc_d = sbuf([P, S], U8, "w2_sc_d", "z2_bf0")
        deal_bytes(w2_sc_d, w2_sc)
        late = planes("late", "yg3")
        for t in range(PACK):
            for piece in whole:
                if t not in EARLY:
                    fetch(late, t, piece, tab_w[t], l_n1)

        got2 = planes("got2", "got4")
        for t in UNFUSED:
            for piece in whole:
                fetch(got2, t, piece, y[t], l_n2)
        diff = planes("diff", "left")
        size = planes("size", "right")
        got7 = planes("got7")

        def make_diff(t, pieces):
            kinds = early if t in EARLY else late
            for piece in pieces:
                if t in UNFUSED:
                    nc.vector.tensor_tensor(diff[:, t, span(*piece)], late[:, t, span(*piece)], got2[:, t, span(*piece)], ALU.add)
                else:
                    fetch_with(diff, t, piece, y[t], l_n2, kinds[:, t, :], ALU.add)
            for piece in pieces:
                at = span(*piece)
                nc.vector.tensor_tensor(diff[:, t, at], y[t][:, at], diff[:, t, at], ALU.subtract)

        def make_size(t, pieces):
            for piece in pieces:
                nc.scalar.activation(size[:, t, span(*piece)], diff[:, t, span(*piece)], ACT.Abs)

        def empty_b(h, u):
            nc.scalar.activation(b[:, 2 * u : 2 * u + 2, cols(h)], b_acc[h, u][:], ACT.Copy, scale=0.0625)

        def fetch_b(t, pieces):
            for piece in pieces:
                fetch(got7_held if t in [0,1,2] else got7, t, piece, b[:, t, :], l_n7)

        make_diff(0, whole)
        make_diff(1, whole)
        for h in range(HALVES):
            make_diff(2, halves[h : h + 1])
            make_diff(3, halves[h : h + 1])
        empty_b(0, 0)
        empty_b(0, 1)
        empty_b(1, 0)
        make_size(0, whole)
        make_size(1, whole)
        empty_b(1, 1)
        for h in range(HALVES):
            make_size(2, halves[h : h + 1])
            make_size(3, halves[h : h + 1])
        got7_held = planes("got7_held", "left")
        fetch_b(0, halves)
        fetch_b(1, halves)
        for h in range(HALVES):
            for t in (2, 3):
                if [t, h] not in [[3,0],[3,1]]:
                    fetch_b(t, halves[h : h + 1])

        z_w = sbuf([P, S], I32, "z_w")
        z_sc = sbuf([P, S], U8, "z_sc")
        z_bf = [sbuf([P, PACK * HALF], BF16, "z_bf%d" % h) for h in range(HALVES)]
        a_acc = {}
        larger = planes("larger")

        def scale_size(h, first, count):
            gn_wide = gn_sb[:].rearrange("p (c t i) -> p c t i", c=1, i=1).to_broadcast([P, count // 4, PACK, 4])
            nc.vector.tensor_tensor(
                woven_by_pairs(z_bf[h][:, span(PACK * first, PACK * count)]),
                by_pairs(size[:, :, span(h * HALF + first, count)]), gn_wide, ALU.mult,
            )

        for h in range(HALVES):
            scale_size(h, 0, HALF)
        for h in range(HALVES):
            quantise(z_w, z_sc, z_bf[h], h)
        got7_late = planes("got7_late", "right")
        for t, h in [[3,0],[3,1]]:
            nc.vector.tensor_copy(got7_late[:, t, cols(h)], b[:, t, :].indirect(part(l_n7, h)))
        for t in range(PACK):
            a_acc[t] = psum.tile([P, S], F32, name="a_acc%d" % t, tag="first%d" % t)
            nc.tensor.matmul_mx(
                a_acc[t][:], lhsT=fp4(w2_w_d, t), lhsT_scale=w2_sc_d[:, block(t)],
                rhs=z_w[:].bitcast(FP8X4), rhs_scale=z_sc[:], start=True, stop=True,
            )

        def make_larger(t):
            where = [got7_late if [t, h] in [[3,0],[3,1]] else got7_held if t in [0,1,2] else got7 for h in range(HALVES)]
            if where[0] is where[1]:
                nc.vector.tensor_tensor(larger[:, t, :], a_acc[t][:], where[0][:, t, :], ALU.max)
            else:
                for h in range(HALVES):
                    nc.vector.tensor_tensor(larger[:, t, cols(h)], a_acc[t][:, cols(h)], where[h][:, t, cols(h)], ALU.max)

        got6 = planes("got6")
        result = planes("result")
        o_w = sbuf([P, S], I32, "o_w")
        o_sc = sbuf([P, S], U8, "o_sc")
        o_bf = [sbuf([P, PACK * HALF], BF16, "o_bf%d" % h) for h in range(HALVES)]
        out_rows = out_0.rearrange("(p t) j -> p t j", t=PACK)
        out_words = out_1[0].rearrange("p n r -> p (n r)").bitcast(I32)

        def fetch_a(t, h):
            if [t, h] in ON_VECTOR:
                nc.vector.tensor_copy(got6[:, t, cols(h)], a[:, t, :].indirect(part(l_n6, h)))
            else:
                fetch(got6, t, halves[h], a[:, t, :], l_n6)

        def empty_a(t):
            empty = nc.vector.tensor_copy if t in [0,2] else nc.scalar.copy
            empty(a[:, t, :], a_acc[t][:])

        def finish(h, first, count, engine):
            some = span(first, count)
            nc.vector.scalar_tensor_tensor(
                got6[:, some, cols(h)], b_acc[h, first // 2][:, span(first % 2, count), :], 0.0625,
                got6[:, some, cols(h)], ALU.mult, ALU.min,
            )
            engine.tensor_tensor(result[:, some, cols(h)], larger[:, some, cols(h)], got6[:, some, cols(h)], ALU.subtract)

        empty_a(0)
        empty_a(1)
        make_larger(0)
        fetch_a(0, 0)
        empty_a(2)
        make_larger(1)
        fetch_a(1, 0)
        empty_a(3)
        make_larger(2)
        fetch_a(2, 0)
        make_larger(3)
        fetch_a(3, 0)
        finish(0, 0, 2, nc.vector)
        finish(0, 2, 2, nc.vector)
        nc.sync.dma_start(out_rows[:, :, cols(0)], result[:, :, cols(0)])
        for t in range(PACK):
            fetch_a(t, 1)
        finish(1, 0, 2, nc.vector)
        nc.sync.dma_start(out_rows[:, :2, cols(1)], result[:, :2, cols(1)])
        finish(1, 2, 1, nc.vector)
        finish(1, 3, 1, nc.vector)
        nc.sync.dma_start(out_rows[:, 2:, cols(1)], result[:, 2:, cols(1)])
        nc.scalar.copy(woven_by_pairs(o_bf[0][:]), by_pairs(result[:, :, cols(0)]))
        nc.vector.tensor_copy(woven_by_pairs(o_bf[1][:]), by_pairs(result[:, :, cols(1)]))
        for h in range(HALVES):
            quantise(o_w, o_sc, o_bf[h], h)
            nc.sync.dma_start(out_words[:, cols(h)], o_w[:, cols(h)])
        for q in range(4):
            queue = nc.scalar if q % 2 == 0 else nc.sync
            queue.dma_start(out_2[0, 4 * q : 4 * q + 4, :].bitcast(I32), o_sc[32 * q : 32 * q + 4, :].bitcast(I32))
